import numpy as np
import ml_dtypes


def mxq(x, axis, fmt="e4m3"):
    dtype, down = {"e4m3": (ml_dtypes.float8_e4m3fn, 7), "e5m2": (ml_dtypes.float8_e5m2, 14)}[fmt]
    v = np.moveaxis(np.asarray(x, np.float32).astype(ml_dtypes.bfloat16).astype(np.float64), axis, -1)
    blocks = v.reshape(v.shape[:-1] + (-1, 32))
    amax = np.abs(blocks).max(-1, keepdims=True)
    byte = np.maximum(np.where(amax > 0, np.frexp(amax)[1] - 1 + 127, 0) - down, 1)
    scale = np.exp2(byte - 127.0)
    codes = (blocks / scale).astype(np.float32).astype(dtype).astype(np.float64)
    return np.moveaxis((codes * scale).reshape(v.shape), -1, axis)


WIDE = False


def mx_kscale(k):
    if not WIDE:
        return np.ones(k)
    levels = np.array([10, -10, 5, -5, 0])
    if k % 512:
        return np.exp2(np.random.permutation(np.resize(levels, k // 32))).repeat(32)
    a = np.empty((k // 512, 16))
    for p in range(k // 512):
        a[p, :8] = np.random.permutation(np.resize(levels, 8))
        for g in range(8):
            far = levels[np.abs(levels - a[p, g]) >= 10]
            a[p, g + 8] = far[np.random.randint(len(far))]
    return np.exp2(a.ravel()).repeat(32)


def f64(x):
    return np.asarray(x).astype(np.float64)


def striped(idx):
    return np.tile(idx.reshape(-1, 16).T, (8, 1)).astype(np.uint16)


def unstriped(offs):
    return offs[:16].T.reshape(-1).astype(np.int64)


E2M1 = np.array([0.0, 0.5, 1.0, 1.5, 2.0, 3.0, 4.0, 6.0, -0.0, -0.5, -1.0, -1.5, -2.0, -3.0, -4.0, -6.0])


def pack_weight(w, fmt):
    k, n = w.shape
    w = f64(np.asarray(w, np.float32).astype(ml_dtypes.bfloat16)).reshape(k // 32, 32, n)
    amax = np.abs(w).max(1)
    if fmt == "e4m3":
        byte = np.frexp(amax)[1] - 1 + 127 - 7
    else:
        mant, ex = np.frexp(amax / 6.0)
        byte = np.where(mant > 0.5, ex, ex - 1) + 127
    byte = np.clip(np.where(amax > 0, byte, 1), 1, 254)
    scaled = (w * np.exp2(127.0 - byte)[:, None, :]).reshape(k, n).astype(np.float32)
    by_word = np.ascontiguousarray(scaled.reshape(k // 512, 128, 4, n).transpose(0, 1, 3, 2))
    if fmt == "e4m3":
        words = by_word.astype(ml_dtypes.float8_e4m3fn).view(np.uint8)
    else:
        c = by_word.astype(ml_dtypes.float4_e2m1fn).view(np.uint8) & 0xF
        words = (c[..., 0::2] | (c[..., 1::2] << 4)).reshape(k // 512, 128, 2 * n)
    return np.ascontiguousarray(words), np.ascontiguousarray(byte.astype(np.uint8).reshape(k // 512, 16, n))


def unpack_weight(words, scales, fmt):
    g, _, n = scales.shape
    words = np.ascontiguousarray(words).reshape(g, 128, n, -1)
    if fmt == "e4m3":
        vals = words.view(ml_dtypes.float8_e4m3fn).astype(np.float64)
    else:
        nib = np.empty((g, 128, n, 4), np.uint8)
        nib[..., 0::2] = words & 0xF
        nib[..., 1::2] = words >> 4
        vals = E2M1[nib]
    vals = vals * np.repeat(np.exp2(scales.astype(np.float64) - 127.0), 8, axis=1)[..., None]
    return vals.transpose(0, 1, 3, 2).reshape(g * 512, n)


def silu(v):
    return v / (1.0 + np.exp(-np.maximum(v, -700.0)))


K, T, E, C, H, N = 512, 512, 8, 256, 512, 128
TOP = 4


def by_expert(wq, xq):
    return np.concatenate([wq[e].T @ xq[:, e * C:(e + 1) * C] for e in range(E)], axis=1)


def setup_inputs():
    n = np.random.standard_normal
    s = mx_kscale(K)[:, None]
    u = mx_kscale(H)
    deal = np.repeat(np.arange(E), C).reshape(TOP, T)[:, np.random.permutation(T)]
    deal = np.take_along_axis(deal, np.argsort(np.random.rand(TOP, T), axis=0), axis=0)
    for _ in range(8):
        s_, t_ = np.random.permutation(T).reshape(2, -1); r = np.random.randint(TOP, size=T // 2); x, y = deal[r, s_].copy(), deal[r, t_].copy()
        ok = ~((deal[:, s_] == y).any(0) | (deal[:, t_] == x).any(0)); deal[r[ok], s_[ok]] = y[ok]; deal[r[ok], t_[ok]] = x[ok]
    order = np.lexsort((np.random.rand(TOP * T), deal.reshape(-1)))
    slot_token = order % T; pos = np.empty(TOP * T, np.int64); pos[order] = np.arange(TOP * T); pos = pos.reshape(TOP, T)
    g = np.random.uniform(0.5, 1.5, (TOP, T)); g = g / g.sum(0)
    w1 = [pack_weight(m, "e2m1") for m in n((E, K, H)) / np.sqrt(K) / s[None]]
    w3 = [pack_weight(m, "e2m1") for m in n((E, K, H)) / np.sqrt(K) / s[None] * u[None, None, :]]
    w2 = [pack_weight(m, "e2m1") for m in n((E, H, N)) / np.sqrt(H) / u[None, :, None]]
    return {
        "xT": (n((K, T)) * s).astype(np.float32),
        "w1_words": np.stack([m[0] for m in w1]),
        "w1_scales": np.stack([m[1] for m in w1]),
        "w3_words": np.stack([m[0] for m in w3]),
        "w3_scales": np.stack([m[1] for m in w3]),
        "w2_words": np.stack([m[0] for m in w2]),
        "w2_scales": np.stack([m[1] for m in w2]),
        "gate": np.stack([np.tile(r, (N, 1)) for r in g]).astype(np.float32),
        "offs": striped(slot_token),
        "pos1": striped(pos[0]),
        "pos2": striped(pos[1]),
        "pos3": striped(pos[2]),
        "pos4": striped(pos[3]),
    }


def reference(xT, w1_words, w1_scales, w3_words, w3_scales, w2_words, w2_scales, gate, offs, pos1, pos2, pos3, pos4):
    idx = unstriped(offs)
    w1 = np.stack([unpack_weight(w1_words[e], w1_scales[e], "e2m1") for e in range(E)])
    w3 = np.stack([unpack_weight(w3_words[e], w3_scales[e], "e2m1") for e in range(E)])
    w2 = np.stack([unpack_weight(w2_words[e], w2_scales[e], "e2m1") for e in range(E)])
    xq = mxq(f64(xT)[:, idx], 0, "e4m3")
    h = silu(by_expert(w1, xq))
    h = h * by_expert(w3, xq)
    y = by_expert(w2, mxq(h, 0, "e4m3"))
    return sum(f64(gate[r]) * y[:, unstriped(p)] for r, p in enumerate((pos1, pos2, pos3, pos4)))

@@ -1,0 +1,245 @@
+from contextlib import ExitStack
+
+import concourse.mybir as mybir
+from concourse.masks import make_identity
+
+T, E, C, K, H, N, TOP = 512, 8, 256, 512, 512, 128, 4
+P = 128
+S = E * C
+FLOPS = 2 * S * (2 * K * H + H * N)
+
+F32 = mybir.dt.float32
+BF16 = mybir.dt.bfloat16
+I32 = mybir.dt.int32
+U32 = mybir.dt.uint32
+U16 = mybir.dt.uint16
+U8 = mybir.dt.uint8
+FP8X4 = mybir.dt.float8_e4m3fn_x4
+FP4X4 = mybir.dt.float4_e2m1fn_x4
+SILU = mybir.ActivationFunctionType.Silu
+ADD = mybir.AluOpType.add
+MULT = mybir.AluOpType.mult
+
+
+def tile_moe_tk_glu_silu_kernel(
+    tc, xT, w1_words, w1_scales, w3_words, w3_scales, w2_words, w2_scales, gate, offs, pos1, pos2, pos3, pos4, out
+):
+    nc = tc.nc
+    with ExitStack() as ctx:
+        keep = ctx.enter_context(tc.tile_pool(name="keep", bufs=1))
+        flow = ctx.enter_context(tc.tile_pool(name="flow", bufs=4))
+        psum_a = ctx.enter_context(tc.psum_pool(name="psum_a", bufs=2))
+        psum_b = ctx.enter_context(tc.psum_pool(name="psum_b", bufs=3))
+        psum_t = ctx.enter_context(tc.psum_pool(name="psum_t", bufs=2))
+        psum_y = ctx.enter_context(tc.psum_pool(name="psum_y", bufs=1))
+
+        offsets = keep.tile([P, S // 16], U16, name="offsets")
+        positions = [keep.tile([P, T // 16], U16, name=f"positions{r}") for r in range(TOP)]
+        x_raw = keep.tile([P, 4, T], F32, name="x_raw")
+        x_rows = keep.tile([P, T, 4], BF16, name="x_rows", align_bytes=64)
+        x_codes = keep.tile([P, T], U32, name="x_codes", align_bytes=64)
+        x_scales = keep.tile([P, T], U8, name="x_scales", align_bytes=64)
+        gates = keep.tile([P, TOP, T], F32, name="gates")
+        y_all = keep.tile([P, S], F32, name="y_all")
+        ident = keep.tile([P, P], F32, name="ident")
+        one = keep.tile([P, 1], F32, name="one")
+
+        groups = [(0, 2), (2, 8)]
+        plane1 = [keep.tile([P, hi - lo, H], U8, name=f"plane1_{lo}", align_bytes=64) for lo, hi in groups]
+        plane3 = [keep.tile([P, hi - lo, H], U8, name=f"plane3_{lo}", align_bytes=64) for lo, hi in groups]
+        plane2 = keep.tile([P, E, N], U8, name="plane2", align_bytes=64)
+        words1 = [keep.tile([P, 2, 2 * H], U8, name=f"words1_{i}", align_bytes=64) for i in range(E // 2)]
+        words3 = [keep.tile([P, 2, 2 * H], U8, name=f"words3_{i}", align_bytes=64) for i in range(E // 2)]
+        words2 = keep.tile([P, E, 2 * N], U8, name="words2", align_bytes=64)
+
+        def zero(plane):
+            nc.vector.memset(plane[:].rearrange("p e i -> p (e i)").bitcast(I32), 0)
+
+        def load_plane(plane, scales, lo, hi):
+            rows = scales.bitcast(I32).rearrange("e s (q r) i -> r q (e s) i", r=4)
+            for r in range(4):
+                nc.sync.dma_start(plane[r:P:32, :, :].bitcast(I32), rows[r][:, lo:hi, :])
+
+        def load_words(tile, words, lo, hi):
+            nc.sync.dma_start(tile[:].bitcast(I32), words.bitcast(I32).rearrange("e s p i -> p (e s) i")[:, lo:hi, :])
+
+        nc.vector.memset(one[:], 0.0)
+        nc.scalar.activation(one[:], one[:], SILU)
+        nc.gpsimd.memset(x_scales[:], 0)
+        zero(plane1[0])
+        zero(plane3[0])
+        zero(plane2)
+        zero(plane1[1])
+        zero(plane3[1])
+        make_identity(nc, ident[:])
+
+        x_view = xT.rearrange("(p j) t -> p j t", j=4)
+        half = T // 2
+        for i in range(2):
+            cols = slice(i * half, (i + 1) * half)
+            nc.sync.dma_start(x_raw[:, :, cols], x_view[:, :, cols])
+        nc.sync.dma_start(offsets[:], offs)
+        load_words(words1[0], w1_words, 0, 2)
+        load_words(words3[0], w3_words, 0, 2)
+        load_plane(plane1[0], w1_scales, 0, 2)
+        load_plane(plane3[0], w3_scales, 0, 2)
+        load_plane(plane2, w2_scales, 0, E)
+        load_words(words2, w2_words, 0, E)
+        load_plane(plane1[1], w1_scales, 2, E)
+        load_plane(plane3[1], w3_scales, 2, E)
+        for i in range(1, E // 2):
+            load_words(words1[i], w1_words, 2 * i, 2 * i + 2)
+            load_words(words3[i], w3_words, 2 * i, 2 * i + 2)
+        for tile, pos in zip(positions, (pos1, pos2, pos3, pos4)):
+            nc.sync.dma_start(tile[:], pos)
+        nc.sync.dma_start(gates[:], gate.rearrange("r p t -> p r t"))
+
+        def interleave(copy, lo, hi):
+            copy(x_rows[:, lo:hi, :], x_raw[:, :, lo:hi].rearrange("p j t -> p t j"))
+
+        def quantise(lo, hi):
+            nc.vector.quantize_mx(
+                out=x_codes[:, lo:hi].bitcast(FP8X4),
+                scales=x_scales[:, lo:hi],
+                in_=x_rows[:, lo:hi, :].rearrange("p t j -> p (t j)"),
+            )
+
+        for i in range(2):
+            lo = i * half
+            interleave(nc.scalar.copy, lo, lo + 128)
+            interleave(nc.vector.tensor_copy, lo + 128, lo + 256)
+            quantise(lo + 128, lo + 256)
+            quantise(lo, lo + 128)
+
+        gathered = {}
+        first = {}
+        hidden = {}
+        turned = {}
+        on_gpsimd = ((0, 1), (1, 1), (2, 1), (4, 1), (5, 1))
+
+        def gather(e):
+            codes = flow.tile([P, C], U32, name="codes", align_bytes=64)
+            scales = flow.tile([P, C], U8, name="scales", align_bytes=64)
+            mine = offsets[:, e * C // 16 : (e + 1) * C // 16]
+            nc.vector.tensor_copy(codes[:], x_codes[:].indirect(mine))
+            nc.vector.tensor_copy(scales[:], x_scales[:].indirect(mine))
+            gathered[e] = (codes, scales)
+
+        def layer1(e):
+            codes, scales = gathered.pop(e)
+            g = 0 if e < 2 else 1
+            k = e - groups[g][0]
+            for s in range(2):
+                cols = slice(s * P, (s + 1) * P)
+                a = psum_a.tile([P, H], F32, name="a")
+                b = psum_b.tile([P, H], F32, name="b")
+                for bank, words, plane in ((a, words1, plane1), (b, words3, plane3)):
+                    nc.tensor.matmul_mx(
+                        out=bank[:],
+                        lhsT=codes[:, cols].bitcast(FP8X4),
+                        lhsT_scale=scales[:, cols],
+                        rhs=words[e // 2][:, e % 2, :].bitcast(FP4X4),
+                        rhs_scale=plane[g][:, k, :],
+                        start=True,
+                        stop=True,
+                    )
+                first[e, s] = (a, b)
+
+        def split(t):
+            return t[:].rearrange("p (m u d) -> p u m d", u=2, d=2)
+
+        def pieces(t):
+            return t[:].rearrange("p (u m d) -> p u m d", u=2, d=2)
+
+        def glu(e, s):
+            a, b = first.pop((e, s))
+            h = flow.tile([P, H], BF16, name="h", align_bytes=64)
+            sa = flow.tile([P, H], F32, name="sa")
+            if (e, s) in on_gpsimd:
+                sb = flow.tile([P, H], F32, name="sb")
+                nc.scalar.copy(pieces(sb), split(b))
+                nc.scalar.activation(pieces(sa), split(a), SILU)
+                nc.gpsimd.tensor_tensor(h[:], sb[:], sa[:], MULT)
+            else:
+                nc.scalar.activation(pieces(sa), split(a), SILU)
+                nc.vector.tensor_tensor(pieces(h), split(b), pieces(sa), MULT)
+            hidden[e, s] = h
+
+        def turn(e, tiles):
+            n = len(tiles)
+            bank = psum_t.tile([P, n, 2, P], F32, name="bank")
+            for i, s in enumerate(tiles):
+                h = hidden.pop((e, s))
+                for u in range(2):
+                    nc.tensor.transpose(bank[:, i, u, :], h[:, u * 256 : (u + 1) * 256].bitcast(F32), ident[:])
+            rows = flow.tile([P, n * P * 4], BF16, name="rows", align_bytes=64)
+            nc.scalar.copy(
+                rows[:].bitcast(F32).rearrange("p (s c u) -> p s c u", s=n, u=2), bank[:].rearrange("p s u c -> p s c u")
+            )
+            turned[e, tiles] = rows
+
+        def layer2(e, tiles):
+            rows = turned.pop((e, tiles))
+            n = len(tiles) * P
+            hc = flow.tile([P, n], U32, name="hc", align_bytes=64)
+            hs = flow.tile([P, n], U8, name="hs", align_bytes=64)
+            nc.vector.quantize_mx(out=hc[:].bitcast(FP8X4), scales=hs[:], in_=rows[:])
+            y = psum_y.tile([P, n], F32, name="y")
+            nc.tensor.matmul_mx(
+                out=y[:],
+                lhsT=words2[:, e, :].bitcast(FP4X4),
+                lhsT_scale=plane2[:, e, :],
+                rhs=hc[:].bitcast(FP8X4),
+                rhs_scale=hs[:],
+                start=True,
+                stop=True,
+            )
+            lo = e * C + tiles[0] * P
+            nc.scalar.copy(y_all[:, lo : lo + n], y[:])
+
+        both = (0, 1)
+        last = E - 1
+        gather(0)
+        layer1(0)
+        gather(1)
+        for e in range(E):
+            if e < last:
+                layer1(e + 1)
+            glu(e, 0)
+            if e == last:
+                turn(last - 1, both)
+            glu(e, 1)
+            if e > 1:
+                layer2(e - 2, both)
+            if e == last:
+                turn(last, (0,))
+                layer2(last - 1, both)
+                turn(last, (1,))
+            elif e > 0:
+                turn(e - 1, both)
+            if e + 2 < E:
+                gather(e + 2)
+        layer2(last, (0,))
+        layer2(last, (1,))
+
+
+        parts = [keep.tile([P, T], F32, name=f"part{r}") for r in range(TOP)]
+
+        def fetch(r):
+            nc.vector.tensor_tensor(parts[r][:], y_all[:].indirect(positions[r][:]), gates[:, r, :], MULT)
+
+        two = keep.tile([P, T], F32, name="two")
+        three = keep.tile([P, T], F32, name="three")
+        total = keep.tile([P, T], F32, name="total")
+        fetch(0)
+        fetch(1)
+        fetch(2)
+        nc.vector.tensor_tensor(two[:], parts[0][:], parts[1][:], ADD)
+        fetch(3)
+        for i in range(2):
+            cols = slice(i * half, (i + 1) * half)
+            nc.vector.tensor_tensor(three[:, cols], two[:, cols], parts[2][:, cols], ADD)
+        for i in range(2):
+            cols = slice(i * half, (i + 1) * half)
+            nc.vector.tensor_tensor(total[:, cols], three[:, cols], parts[3][:, cols], ADD)
+            nc.sync.dma_start(out[:, cols], total[:, cols])

@@ -44,9 +44,8 @@ def tile_moe_tk_glu_silu_kernel(
         ident = keep.tile([P, P], F32, name="ident")
         one = keep.tile([P, 1], F32, name="one")
 
-        groups = [(0, 2), (2, 8)]
-        plane1 = [keep.tile([P, hi - lo, H], U8, name=f"plane1_{lo}", align_bytes=64) for lo, hi in groups]
-        plane3 = [keep.tile([P, hi - lo, H], U8, name=f"plane3_{lo}", align_bytes=64) for lo, hi in groups]
+        plane1 = keep.tile([P, E, H], U8, name="plane1", align_bytes=64)
+        plane3 = keep.tile([P, E, H], U8, name="plane3", align_bytes=64)
         plane2 = keep.tile([P, E, N], U8, name="plane2", align_bytes=64)
         words1 = [keep.tile([P, 2, 2 * H], U8, name=f"words1_{i}", align_bytes=64) for i in range(E // 2)]
         words3 = [keep.tile([P, 2, 2 * H], U8, name=f"words3_{i}", align_bytes=64) for i in range(E // 2)]
@@ -63,31 +62,28 @@ def tile_moe_tk_glu_silu_kernel(
         def load_words(tile, words, lo, hi):
             nc.sync.dma_start(tile[:].bitcast(I32), words.bitcast(I32).rearrange("e s p i -> p (e s) i")[:, lo:hi, :])
 
-        nc.vector.memset(one[:], 0.0)
-        nc.scalar.activation(one[:], one[:], SILU)
-        nc.gpsimd.memset(x_scales[:], 0)
-        zero(plane1[0])
-        zero(plane3[0])
-        zero(plane2)
-        zero(plane1[1])
-        zero(plane3[1])
-        make_identity(nc, ident[:])
-
         x_view = xT.rearrange("(p j) t -> p j t", j=4)
         half = T // 2
         for i in range(2):
             cols = slice(i * half, (i + 1) * half)
             nc.sync.dma_start(x_raw[:, :, cols], x_view[:, :, cols])
         nc.sync.dma_start(offsets[:], offs)
+        nc.vector.memset(one[:], 0.0)
+        nc.scalar.activation(one[:], one[:], SILU)
+        zero(plane1)
+        zero(plane3)
+        zero(plane2)
+        nc.gpsimd.memset(x_scales[:], 0)
+        make_identity(nc, ident[:])
         load_words(words1[0], w1_words, 0, 2)
         load_words(words3[0], w3_words, 0, 2)
-        load_plane(plane1[0], w1_scales, 0, 2)
-        load_plane(plane3[0], w3_scales, 0, 2)
+        load_plane(plane1, w1_scales, 0, E)
+        load_plane(plane3, w3_scales, 0, E)
+        load_words(words1[1], w1_words, 2, 4)
+        load_words(words3[1], w3_words, 2, 4)
         load_plane(plane2, w2_scales, 0, E)
         load_words(words2, w2_words, 0, E)
-        load_plane(plane1[1], w1_scales, 2, E)
-        load_plane(plane3[1], w3_scales, 2, E)
-        for i in range(1, E // 2):
+        for i in range(2, E // 2):
             load_words(words1[i], w1_words, 2 * i, 2 * i + 2)
             load_words(words3[i], w3_words, 2 * i, 2 * i + 2)
         for tile, pos in zip(positions, (pos1, pos2, pos3, pos4)):
@@ -115,7 +111,7 @@ def tile_moe_tk_glu_silu_kernel(
         first = {}
         hidden = {}
         turned = {}
-        on_gpsimd = ((0, 1), (1, 1), (2, 1), (4, 1), (5, 1))
+        on_gpsimd = ()
 
         def gather(e):
             codes = flow.tile([P, C], U32, name="codes", align_bytes=64)
@@ -125,25 +121,22 @@ def tile_moe_tk_glu_silu_kernel(
             nc.vector.tensor_copy(scales[:], x_scales[:].indirect(mine))
             gathered[e] = (codes, scales)
 
-        def layer1(e):
-            codes, scales = gathered.pop(e)
-            g = 0 if e < 2 else 1
-            k = e - groups[g][0]
-            for s in range(2):
-                cols = slice(s * P, (s + 1) * P)
-                a = psum_a.tile([P, H], F32, name="a")
-                b = psum_b.tile([P, H], F32, name="b")
-                for bank, words, plane in ((a, words1, plane1), (b, words3, plane3)):
-                    nc.tensor.matmul_mx(
-                        out=bank[:],
-                        lhsT=codes[:, cols].bitcast(FP8X4),
-                        lhsT_scale=scales[:, cols],
-                        rhs=words[e // 2][:, e % 2, :].bitcast(FP4X4),
-                        rhs_scale=plane[g][:, k, :],
-                        start=True,
-                        stop=True,
-                    )
-                first[e, s] = (a, b)
+        def layer1(e, s):
+            codes, scales = gathered[e]
+            cols = slice(s * P, (s + 1) * P)
+            a = psum_a.tile([P, H], F32, name="a")
+            b = psum_b.tile([P, H], F32, name="b")
+            for bank, words, plane in ((a, words1, plane1), (b, words3, plane3)):
+                nc.tensor.matmul_mx(
+                    out=bank[:],
+                    lhsT=codes[:, cols].bitcast(FP8X4),
+                    lhsT_scale=scales[:, cols],
+                    rhs=words[e // 2][:, e % 2, :].bitcast(FP4X4),
+                    rhs_scale=plane[:, e, :],
+                    start=True,
+                    stop=True,
+                )
+            first[e, s] = (a, b)
 
         def split(t):
             return t[:].rearrange("p (m u d) -> p u m d", u=2, d=2)
@@ -199,29 +192,30 @@ def tile_moe_tk_glu_silu_kernel(
 
         both = (0, 1)
         last = E - 1
+        tiles = 2 * E
         gather(0)
-        layer1(0)
+        layer1(0, 0)
+        layer1(0, 1)
         gather(1)
-        for e in range(E):
-            if e < last:
-                layer1(e + 1)
-            glu(e, 0)
-            if e == last:
-                turn(last - 1, both)
-            glu(e, 1)
-            if e > 1:
-                layer2(e - 2, both)
-            if e == last:
-                turn(last, (0,))
-                layer2(last - 1, both)
-                turn(last, (1,))
-            elif e > 0:
-                turn(e - 1, both)
-            if e + 2 < E:
-                gather(e + 2)
+        for t in range(tiles):
+            if t + 2 < tiles:
+                layer1((t + 2) // 2, (t + 2) % 2)
+            glu(t // 2, t % 2)
+            if t % 2 == 0 and t // 2 + 2 < E:
+                gather(t // 2 + 2)
+            if t == tiles - 1:
+                break
+            u = t - 1
+            if u > 0 and u % 2 == 1:
+                turn(u // 2, both)
+            v = t - 3
+            if v > 0 and v % 2 == 1:
+                layer2(v // 2, both)
+        turn(last, (0,))
+        layer2(6, both)
+        turn(last, (1,))
         layer2(last, (0,))
         layer2(last, (1,))
-
 
         parts = [keep.tile([P, T], F32, name=f"part{r}") for r in range(TOP)]
 

@@ -75,9 +75,9 @@ def tile_moe_tk_glu_silu_kernel(
         zero(plane2)
         nc.gpsimd.memset(x_scales[:], 0)
         make_identity(nc, ident[:])
+        load_plane(plane1, w1_scales, 0, E)
         load_words(words1[0], w1_words, 0, 2)
         load_words(words3[0], w3_words, 0, 2)
-        load_plane(plane1, w1_scales, 0, E)
         load_plane(plane3, w3_scales, 0, E)
         load_words(words1[1], w1_words, 2, 4)
         load_words(words3[1], w3_words, 2, 4)
@@ -100,37 +100,43 @@ def tile_moe_tk_glu_silu_kernel(
                 in_=x_rows[:, lo:hi, :].rearrange("p t j -> p (t j)"),
             )
 
-        for i in range(2):
-            lo = i * half
-            interleave(nc.scalar.copy, lo, lo + 128)
-            interleave(nc.vector.tensor_copy, lo + 128, lo + 256)
-            quantise(lo + 128, lo + 256)
-            quantise(lo, lo + 128)
+        interleave(nc.scalar.copy, 0, 128)
+        interleave(nc.vector.tensor_copy, 128, 256)
+        quantise(128, 256)
+        quantise(0, 128)
+        interleave(nc.scalar.copy, 448, 512)
+        interleave(nc.vector.tensor_copy, 256, 384)
+        interleave(nc.vector.tensor_copy, 384, 448)
+        quantise(256, 384)
+        quantise(384, 512)
 
         gathered = {}
+        runs = [(0, 128), (128, 512), (512, 896), (896, 1280), (1280, 1664), (1664, 2048)]
         first = {}
         hidden = {}
         turned = {}
         on_gpsimd = ()
 
-        def gather(e):
-            codes = flow.tile([P, C], U32, name="codes", align_bytes=64)
-            scales = flow.tile([P, C], U8, name="scales", align_bytes=64)
-            mine = offsets[:, e * C // 16 : (e + 1) * C // 16]
+        def gather(g):
+            lo, hi = runs[g]
+            codes = flow.tile([P, hi - lo], U32, name="codes", align_bytes=64)
+            scales = flow.tile([P, hi - lo], U8, name="scales", align_bytes=64)
+            mine = offsets[:, lo // 16 : hi // 16]
             nc.vector.tensor_copy(codes[:], x_codes[:].indirect(mine))
             nc.vector.tensor_copy(scales[:], x_scales[:].indirect(mine))
-            gathered[e] = (codes, scales)
+            for t in range(lo // P, hi // P):
+                cols = slice(t * P - lo, t * P - lo + P)
+                gathered[t] = (codes[:, cols], scales[:, cols])
 
         def layer1(e, s):
-            codes, scales = gathered[e]
-            cols = slice(s * P, (s + 1) * P)
+            codes, scales = gathered.pop(2 * e + s)
             a = psum_a.tile([P, H], F32, name="a")
             b = psum_b.tile([P, H], F32, name="b")
             for bank, words, plane in ((a, words1, plane1), (b, words3, plane3)):
                 nc.tensor.matmul_mx(
                     out=bank[:],
-                    lhsT=codes[:, cols].bitcast(FP8X4),
-                    lhsT_scale=scales[:, cols],
+                    lhsT=codes.bitcast(FP8X4),
+                    lhsT_scale=scales,
                     rhs=words[e // 2][:, e % 2, :].bitcast(FP4X4),
                     rhs_scale=plane[:, e, :],
                     start=True,
@@ -158,7 +164,7 @@ def tile_moe_tk_glu_silu_kernel(
                 nc.vector.tensor_tensor(pieces(h), split(b), pieces(sa), MULT)
             hidden[e, s] = h
 
-        def turn(e, tiles):
+        def turn(e, tiles, copy):
             n = len(tiles)
             bank = psum_t.tile([P, n, 2, P], F32, name="bank")
             for i, s in enumerate(tiles):
@@ -166,18 +172,18 @@ def tile_moe_tk_glu_silu_kernel(
                 for u in range(2):
                     nc.tensor.transpose(bank[:, i, u, :], h[:, u * 256 : (u + 1) * 256].bitcast(F32), ident[:])
             rows = flow.tile([P, n * P * 4], BF16, name="rows", align_bytes=64)
-            nc.scalar.copy(
+            copy(
                 rows[:].bitcast(F32).rearrange("p (s c u) -> p s c u", s=n, u=2), bank[:].rearrange("p s u c -> p s c u")
             )
             turned[e, tiles] = rows
 
-        def layer2(e, tiles):
+        def layer2(e, tiles, pool, name, copy):
             rows = turned.pop((e, tiles))
             n = len(tiles) * P
             hc = flow.tile([P, n], U32, name="hc", align_bytes=64)
             hs = flow.tile([P, n], U8, name="hs", align_bytes=64)
             nc.vector.quantize_mx(out=hc[:].bitcast(FP8X4), scales=hs[:], in_=rows[:])
-            y = psum_y.tile([P, n], F32, name="y")
+            y = pool.tile([P, n], F32, name=name)
             nc.tensor.matmul_mx(
                 out=y[:],
                 lhsT=words2[:, e, :].bitcast(FP4X4),
@@ -188,34 +194,37 @@ def tile_moe_tk_glu_silu_kernel(
                 stop=True,
             )
             lo = e * C + tiles[0] * P
-            nc.scalar.copy(y_all[:, lo : lo + n], y[:])
+            copy(y_all[:, lo : lo + n], y[:])
 
         both = (0, 1)
         last = E - 1
         tiles = 2 * E
+        scalar_copy = nc.scalar.copy
+        vector_copy = nc.vector.tensor_copy
         gather(0)
         layer1(0, 0)
-        layer1(0, 1)
         gather(1)
+        layer1(0, 1)
+        gather(2)
+        ahead = 3
         for t in range(tiles):
             if t + 2 < tiles:
                 layer1((t + 2) // 2, (t + 2) % 2)
             glu(t // 2, t % 2)
-            if t % 2 == 0 and t // 2 + 2 < E:
-                gather(t // 2 + 2)
-            if t == tiles - 1:
-                break
-            u = t - 1
-            if u > 0 and u % 2 == 1:
-                turn(u // 2, both)
-            v = t - 3
-            if v > 0 and v % 2 == 1:
-                layer2(v // 2, both)
-        turn(last, (0,))
-        layer2(6, both)
-        turn(last, (1,))
-        layer2(last, (0,))
-        layer2(last, (1,))
+            if ahead < len(runs) and runs[ahead][0] <= (t + 5) * P:
+                gather(ahead)
+                ahead += 1
+            if t > 1 and t % 2 == 0:
+                turn(t // 2 - 1, both, scalar_copy)
+            if t == tiles - 2:
+                turn(last, (0,), scalar_copy)
+            elif t > 3 and t % 2 == 0:
+                layer2(t // 2 - 2, both, psum_y, "y", scalar_copy)
+        turn(last, (1,), vector_copy)
+        layer2(last - 2, both, psum_y, "y", scalar_copy)
+        layer2(last - 1, both, psum_a, "a", scalar_copy)
+        layer2(last, (0,), psum_a, "a", scalar_copy)
+        layer2(last, (1,), psum_y, "y", vector_copy)
 
         parts = [keep.tile([P, T], F32, name=f"part{r}") for r in range(TOP)]
 
@@ -230,10 +239,9 @@ def tile_moe_tk_glu_silu_kernel(
         fetch(2)
         nc.vector.tensor_tensor(two[:], parts[0][:], parts[1][:], ADD)
         fetch(3)
-        for i in range(2):
-            cols = slice(i * half, (i + 1) * half)
+        pieces3 = (slice(0, 256), slice(256, 512))
+        for cols in pieces3:
             nc.vector.tensor_tensor(three[:, cols], two[:, cols], parts[2][:, cols], ADD)
-        for i in range(2):
-            cols = slice(i * half, (i + 1) * half)
+        for cols in (slice(0, 256), slice(256, 384), slice(384, 512)):
             nc.vector.tensor_tensor(total[:, cols], three[:, cols], parts[3][:, cols], ADD)
             nc.sync.dma_start(out[:, cols], total[:, cols])

from contextlib import ExitStack

import concourse.mybir as mybir
from concourse.masks import make_identity

T, E, C, K, H, N, TOP = 512, 8, 256, 512, 512, 128, 4
P = 128
S = E * C
FLOPS = 2 * S * (2 * K * H + H * N)

F32 = mybir.dt.float32
BF16 = mybir.dt.bfloat16
I32 = mybir.dt.int32
U32 = mybir.dt.uint32
U16 = mybir.dt.uint16
U8 = mybir.dt.uint8
FP8X4 = mybir.dt.float8_e4m3fn_x4
FP4X4 = mybir.dt.float4_e2m1fn_x4
SILU = mybir.ActivationFunctionType.Silu
ADD = mybir.AluOpType.add
MULT = mybir.AluOpType.mult


def tile_moe_tk_glu_silu_kernel(
    tc, xT, w1_words, w1_scales, w3_words, w3_scales, w2_words, w2_scales, gate, offs, pos1, pos2, pos3, pos4, out
):
    nc = tc.nc
    with ExitStack() as ctx:
        keep = ctx.enter_context(tc.tile_pool(name="keep", bufs=1))
        flow = ctx.enter_context(tc.tile_pool(name="flow", bufs=4))
        psum_a = ctx.enter_context(tc.psum_pool(name="psum_a", bufs=2))
        psum_b = ctx.enter_context(tc.psum_pool(name="psum_b", bufs=3))
        psum_t = ctx.enter_context(tc.psum_pool(name="psum_t", bufs=2))
        psum_y = ctx.enter_context(tc.psum_pool(name="psum_y", bufs=1))

        offsets = keep.tile([P, S // 16], U16, name="offsets")
        positions = [keep.tile([P, T // 16], U16, name=f"positions{r}") for r in range(TOP)]
        x_raw = keep.tile([P, 4, T], F32, name="x_raw")
        x_rows = keep.tile([P, T, 4], BF16, name="x_rows", align_bytes=64)
        x_codes = keep.tile([P, T], U32, name="x_codes", align_bytes=64)
        x_scales = keep.tile([P, T], U8, name="x_scales", align_bytes=64)
        gates = keep.tile([P, TOP, T], F32, name="gates")
        y_all = keep.tile([P, S], F32, name="y_all")
        ident = keep.tile([P, P], F32, name="ident")
        one = keep.tile([P, 1], F32, name="one")

        plane1 = keep.tile([P, E, H], U8, name="plane1", align_bytes=64)
        plane3 = keep.tile([P, E, H], U8, name="plane3", align_bytes=64)
        plane2 = keep.tile([P, E, N], U8, name="plane2", align_bytes=64)
        words1 = [keep.tile([P, 2, 2 * H], U8, name=f"words1_{i}", align_bytes=64) for i in range(E // 2)]
        words3 = [keep.tile([P, 2, 2 * H], U8, name=f"words3_{i}", align_bytes=64) for i in range(E // 2)]
        words2 = keep.tile([P, E, 2 * N], U8, name="words2", align_bytes=64)

        def zero(plane):
            nc.vector.memset(plane[:].rearrange("p e i -> p (e i)").bitcast(I32), 0)

        def load_plane(plane, scales, lo, hi):
            rows = scales.bitcast(I32).rearrange("e s (q r) i -> r q (e s) i", r=4)
            for r in range(4):
                nc.sync.dma_start(plane[r:P:32, :, :].bitcast(I32), rows[r][:, lo:hi, :])

        def load_words(tile, words, lo, hi):
            nc.sync.dma_start(tile[:].bitcast(I32), words.bitcast(I32).rearrange("e s p i -> p (e s) i")[:, lo:hi, :])

        x_view = xT.rearrange("(p j) t -> p j t", j=4)
        half = T // 2
        for i in range(2):
            cols = slice(i * half, (i + 1) * half)
            nc.sync.dma_start(x_raw[:, :, cols], x_view[:, :, cols])
        nc.sync.dma_start(offsets[:], offs)
        nc.vector.memset(one[:], 0.0)
        nc.scalar.activation(one[:], one[:], SILU)
        zero(plane1)
        zero(plane3)
        zero(plane2)
        nc.gpsimd.memset(x_scales[:], 0)
        make_identity(nc, ident[:])
        load_plane(plane1, w1_scales, 0, E)
        load_words(words1[0], w1_words, 0, 2)
        load_words(words3[0], w3_words, 0, 2)
        load_plane(plane3, w3_scales, 0, E)
        load_words(words1[1], w1_words, 2, 4)
        load_words(words3[1], w3_words, 2, 4)
        load_plane(plane2, w2_scales, 0, E)
        load_words(words2, w2_words, 0, E)
        for i in range(2, E // 2):
            load_words(words1[i], w1_words, 2 * i, 2 * i + 2)
            load_words(words3[i], w3_words, 2 * i, 2 * i + 2)
        for tile, pos in zip(positions, (pos1, pos2, pos3, pos4)):
            nc.sync.dma_start(tile[:], pos)
        nc.sync.dma_start(gates[:], gate.rearrange("r p t -> p r t"))

        def interleave(copy, lo, hi):
            copy(x_rows[:, lo:hi, :], x_raw[:, :, lo:hi].rearrange("p j t -> p t j"))

        def quantise(lo, hi):
            nc.vector.quantize_mx(
                out=x_codes[:, lo:hi].bitcast(FP8X4),
                scales=x_scales[:, lo:hi],
                in_=x_rows[:, lo:hi, :].rearrange("p t j -> p (t j)"),
            )

        interleave(nc.scalar.copy, 0, 128)
        interleave(nc.vector.tensor_copy, 128, 256)
        quantise(128, 256)
        quantise(0, 128)
        interleave(nc.scalar.copy, 448, 512)
        interleave(nc.vector.tensor_copy, 256, 384)
        interleave(nc.vector.tensor_copy, 384, 448)
        quantise(256, 384)
        quantise(384, 512)

        gathered = {}
        runs = [(0, 128), (128, 512), (512, 896), (896, 1280), (1280, 1664), (1664, 2048)]
        first = {}
        hidden = {}
        turned = {}
        on_gpsimd = ()

        def gather(g):
            lo, hi = runs[g]
            codes = flow.tile([P, hi - lo], U32, name="codes", align_bytes=64)
            scales = flow.tile([P, hi - lo], U8, name="scales", align_bytes=64)
            mine = offsets[:, lo // 16 : hi // 16]
            nc.vector.tensor_copy(codes[:], x_codes[:].indirect(mine))
            nc.vector.tensor_copy(scales[:], x_scales[:].indirect(mine))
            for t in range(lo // P, hi // P):
                cols = slice(t * P - lo, t * P - lo + P)
                gathered[t] = (codes[:, cols], scales[:, cols])

        def layer1(e, s):
            codes, scales = gathered.pop(2 * e + s)
            a = psum_a.tile([P, H], F32, name="a")
            b = psum_b.tile([P, H], F32, name="b")
            for bank, words, plane in ((a, words1, plane1), (b, words3, plane3)):
                nc.tensor.matmul_mx(
                    out=bank[:],
                    lhsT=codes.bitcast(FP8X4),
                    lhsT_scale=scales,
                    rhs=words[e // 2][:, e % 2, :].bitcast(FP4X4),
                    rhs_scale=plane[:, e, :],
                    start=True,
                    stop=True,
                )
            first[e, s] = (a, b)

        def split(t):
            return t[:].rearrange("p (m u d) -> p u m d", u=2, d=2)

        def pieces(t):
            return t[:].rearrange("p (u m d) -> p u m d", u=2, d=2)

        def glu(e, s):
            a, b = first.pop((e, s))
            h = flow.tile([P, H], BF16, name="h", align_bytes=64)
            sa = flow.tile([P, H], F32, name="sa")
            if (e, s) in on_gpsimd:
                sb = flow.tile([P, H], F32, name="sb")
                nc.scalar.copy(pieces(sb), split(b))
                nc.scalar.activation(pieces(sa), split(a), SILU)
                nc.gpsimd.tensor_tensor(h[:], sb[:], sa[:], MULT)
            else:
                nc.scalar.activation(pieces(sa), split(a), SILU)
                nc.vector.tensor_tensor(pieces(h), split(b), pieces(sa), MULT)
            hidden[e, s] = h

        def turn(e, tiles, copy):
            n = len(tiles)
            bank = psum_t.tile([P, n, 2, P], F32, name="bank")
            for i, s in enumerate(tiles):
                h = hidden.pop((e, s))
                for u in range(2):
                    nc.tensor.transpose(bank[:, i, u, :], h[:, u * 256 : (u + 1) * 256].bitcast(F32), ident[:])
            rows = flow.tile([P, n * P * 4], BF16, name="rows", align_bytes=64)
            copy(
                rows[:].bitcast(F32).rearrange("p (s c u) -> p s c u", s=n, u=2), bank[:].rearrange("p s u c -> p s c u")
            )
            turned[e, tiles] = rows

        def layer2(e, tiles, pool, name, copy):
            rows = turned.pop((e, tiles))
            n = len(tiles) * P
            hc = flow.tile([P, n], U32, name="hc", align_bytes=64)
            hs = flow.tile([P, n], U8, name="hs", align_bytes=64)
            nc.vector.quantize_mx(out=hc[:].bitcast(FP8X4), scales=hs[:], in_=rows[:])
            y = pool.tile([P, n], F32, name=name)
            nc.tensor.matmul_mx(
                out=y[:],
                lhsT=words2[:, e, :].bitcast(FP4X4),
                lhsT_scale=plane2[:, e, :],
                rhs=hc[:].bitcast(FP8X4),
                rhs_scale=hs[:],
                start=True,
                stop=True,
            )
            lo = e * C + tiles[0] * P
            copy(y_all[:, lo : lo + n], y[:])

        both = (0, 1)
        last = E - 1
        tiles = 2 * E
        scalar_copy = nc.scalar.copy
        vector_copy = nc.vector.tensor_copy
        gather(0)
        layer1(0, 0)
        gather(1)
        layer1(0, 1)
        gather(2)
        ahead = 3
        for t in range(tiles):
            if t + 2 < tiles:
                layer1((t + 2) // 2, (t + 2) % 2)
            glu(t // 2, t % 2)
            if ahead < len(runs) and runs[ahead][0] <= (t + 5) * P:
                gather(ahead)
                ahead += 1
            if t > 1 and t % 2 == 0:
                turn(t // 2 - 1, both, scalar_copy)
            if t == tiles - 2:
                turn(last, (0,), scalar_copy)
            elif t > 3 and t % 2 == 0:
                layer2(t // 2 - 2, both, psum_y, "y", scalar_copy)
        turn(last, (1,), vector_copy)
        layer2(last - 2, both, psum_y, "y", scalar_copy)
        layer2(last - 1, both, psum_a, "a", scalar_copy)
        layer2(last, (0,), psum_a, "a", scalar_copy)
        layer2(last, (1,), psum_y, "y", vector_copy)

        parts = [keep.tile([P, T], F32, name=f"part{r}") for r in range(TOP)]

        def fetch(r):
            nc.vector.tensor_tensor(parts[r][:], y_all[:].indirect(positions[r][:]), gates[:, r, :], MULT)

        two = keep.tile([P, T], F32, name="two")
        three = keep.tile([P, T], F32, name="three")
        total = keep.tile([P, T], F32, name="total")
        fetch(0)
        fetch(1)
        fetch(2)
        nc.vector.tensor_tensor(two[:], parts[0][:], parts[1][:], ADD)
        fetch(3)
        pieces3 = (slice(0, 256), slice(256, 512))
        for cols in pieces3:
            nc.vector.tensor_tensor(three[:, cols], two[:, cols], parts[2][:, cols], ADD)
        for cols in (slice(0, 256), slice(256, 384), slice(384, 512)):
            nc.vector.tensor_tensor(total[:, cols], three[:, cols], parts[3][:, cols], ADD)
            nc.sync.dma_start(out[:, cols], total[:, cols])
